import numpy as np, ml_dtypes
CORES = [2,6,26,30,66,70,74,78,82,86]
N = 10
TOK, CAP, FF = 256, 48, 4
def entries(a): return a.T.reshape(-1)
def pack(v, P): return np.ascontiguousarray(np.asarray(v, np.int32).reshape(-1, P).T)
def lists(rng, how):
    E = rng.integers(0, N, (N, TOK))
    if how == "hot": E[:] = rng.integers(N)
    if how == "none": E = (int(rng.integers(N)) + 1 + rng.integers(0, N - 1, (N, TOK))) % N
    if how == "skew": E = np.where(rng.random((N, TOK)) < 0.7, rng.integers(0, N, (N, 1)), E)
    if how == "even": E = np.stack([rng.permutation(np.arange(TOK) % N) for r in range(N)])
    if how == "own": E = np.repeat(np.arange(N).reshape(N, 1), TOK, axis=1)
    return {"ex": np.stack([pack(E[r], 16) for r in range(N)])}
def setup_inputs(rng):
    return dict({"x": rng.standard_normal((N, 128, TOK), dtype=np.float32).astype(ml_dtypes.bfloat16), "w1": (rng.standard_normal((N, 128, FF * 128), dtype=np.float32) / 8).astype(ml_dtypes.bfloat16), "w2": (rng.standard_normal((N, 128, FF * 128), dtype=np.float32) / 16).astype(ml_dtypes.bfloat16)}, **lists(rng, "uniform"))
def setup_inputs_even(rng):
    d = setup_inputs(rng); d.update(lists(rng, "even"))
    for k in ("x",): d[k] = (d[k].astype(np.float32) * 1024.0).astype(d[k].dtype)
    return d
def setup_inputs_hot(rng):
    d = setup_inputs(rng); d.update(lists(rng, "hot"))
    for k in ("x",): d[k] = (d[k].astype(np.float32) * (1 / 1024.0)).astype(d[k].dtype)
    return d
def setup_inputs_none(rng):
    d = setup_inputs(rng); d.update(lists(rng, "none"))
    return d
def setup_inputs_own(rng):
    d = setup_inputs(rng); d.update(lists(rng, "own"))
    return d
def setup_inputs_skew(rng):
    d = setup_inputs(rng); d.update(lists(rng, "skew"))
    return d
def check_inputs(x):
    bad = []
    if x["ex"].min() < 0 or x["ex"].max() >= N: bad.append("ex out of range")
    return bad
def reference(x, w1, w2, ex):
    X, W1, W2 = x.astype(np.float64), w1.astype(np.float64), w2.astype(np.float64)
    y = np.zeros((N, 128, TOK))
    for r in range(N):
        E = entries(ex[r]); place = np.array([np.sum(E[:t] == E[t]) for t in range(TOK)])
        for k in range(N):
            m = (E == k) & (place < CAP)
            y[r][:, m] = sum(W2[k][:, 128 * f:128 * f + 128].T @ np.maximum(W1[k][:, 128 * f:128 * f + 128].T @ X[r][:, m], 0.0) for f in range(FF))
    return {"y": y.astype(ml_dtypes.bfloat16)}

@@ -1,0 +1,317 @@
+import numpy as np
+from concourse.bass import DstId, RemoteDMATransfer
+from concourse.mybir import AluOpType, ActivationFunctionType
+
+HELPERS = True
+CAP, TOK, FF = 48, 256, 4
+BLK = 2 * CAP
+GAP = TOK - CAP
+STR = BLK + GAP
+NCH = 5
+WIN = GAP + NCH * STR
+
+SCRATCH = {
+    "E": ("sbuf", [128, 16], "int32"),
+    "xs": ("sbuf", [128, TOK], "bfloat16"),
+    "w": ("sbuf", [128, 2048], "bfloat16"),
+    "send": ("sbuf", [128, WIN], "bfloat16"),
+    "ret": ("sbuf", [128, WIN], "bfloat16"),
+    "land": ("sbuf", [128, 4 * BLK], "bfloat16"),
+    "outb": ("sbuf", [128, 4 * BLK], "bfloat16"),
+    "hs": ("sbuf", [128, 4 * 192], "bfloat16"),
+    "ysb": ("sbuf", [128, TOK], "bfloat16"),
+    "off": ("sbuf", [128, 16], "uint16"),
+    "pcol": ("sbuf", [128, 1], "int32"),
+    "icol": ("sbuf", [128, 4], "int32"),
+    "cols": ("sbuf", [128, 8], "float32"),
+    "gfree": ("sbuf", [128, 128], "bfloat16"),
+    "vfree": ("sbuf", [128, 128], "bfloat16"),
+    "afree": ("sbuf", [128, 128], "bfloat16"),
+    "blk": ("sbuf", [128, 128], "bfloat16"),
+    "pos": ("sbuf", [128, 128], "bfloat16"),
+    "tri": ("sbuf", [128, 128], "bfloat16"),
+    "rest": ("sbuf", [128, 128], "bfloat16"),
+    "sel": ("sbuf", [128, 128], "bfloat16"),
+    "mask": ("sbuf", [128, 40], "float32"),
+    "oh": ("sbuf", [128, 40], "bfloat16"),
+    "ohb": ("sbuf", [128, 32], "bfloat16"),
+    "wsc": ("sbuf", [128, 40], "float32"),
+    "val": ("sbuf", [128, 40], "bfloat16"),
+    "pd": ("psum", [128, 512], "float32"),
+    "po": ("psum", [128, 512], "float32"),
+    "ph00": ("psum", [128, 512], "float32"),
+    "ph01": ("psum", [128, 512], "float32"),
+    "ph10": ("psum", [128, 512], "float32"),
+    "ph11": ("psum", [128, 512], "float32"),
+    "py0": ("psum", [128, 512], "float32"),
+    "py1": ("psum", [128, 512], "float32"),
+}
+SEMAPHORES = ["cv", "cs", "cp", "cg", "lde", "ldx", "w10", "w11", "w20", "w21",
+              "ar1", "ar2", "ar3", "ar4", "back", "sent", "st"]
+
+
+def _bits(m):
+    return bin(m).count("1")
+
+
+def _plan(T, topo):
+    cores = list(T.cores)
+    chips = []
+    for c in cores:
+        if topo.chip(c) not in chips:
+            chips.append(topo.chip(c))
+    assert len(chips) == NCH
+    on = [[c for c in cores if topo.chip(c) == ch] for ch in chips]
+    for j in range(NCH):
+        assert len(on[j]) == 2 and cores.index(on[j][0]) == 2 * j and cores.index(on[j][1]) == 2 * j + 1
+        assert topo.die(on[j][0]) != topo.die(on[j][1])
+    lane = {}
+    for j in range(NCH):
+        for c in on[j]:
+            lane[(j, topo.die(c))] = c
+    helper = {}
+    if HELPERS:
+        for j in range(NCH):
+            for c in on[j]:
+                d = topo.die(c)
+                for h in range(min(on[j]) - 8, max(on[j]) + 8):
+                    if h < 0 or h in cores or topo.chip(h) != chips[j] or topo.die(h) != d:
+                        continue
+                    if all(topo.may_write(h, lane[(i, d)]) for i in range(NCH) if i != j):
+                        helper[c] = h
+                        break
+                assert c in helper
+    return cores, chips, on, lane, helper
+
+
+def rank_program(g, core, T, topo):
+    cores, chips, on, lane, helper = _plan(T, topo)
+    is_rank = core in cores
+    owner = core if is_rank else None
+    for c in helper:
+        if helper[c] == core:
+            owner = c
+    if owner is None:
+        return
+    j = chips.index(topo.chip(core))
+    die = topo.die(core)
+    side = on[j].index(owner)
+
+    def worker(ch, s):
+        r = lane[(ch, die)]
+        return helper[r] if (HELPERS and s % 2 == 1) else r
+
+    my_rounds = [s for s in range(1, NCH) if worker(j, s) == core]
+
+    Q = {"v": g.vector, "s": g.scalar, "p": g.tensor, "g": g, "y": g.sync}
+    cnt = {"cv": 0, "cs": 0, "cp": 0, "cg": 0}
+    total = {}
+    seen = {}
+
+    def done(q, ins):
+        s = "c" + q
+        ins.then_inc(T.sem[s], 1)
+        cnt[s] += 1
+        total[s] = cnt[s]
+        return (s, cnt[s])
+
+    def need(q, *tickets):
+        for t in tickets:
+            if t is None:
+                continue
+            s, v = t
+            if seen.get((q, s), 0) < v:
+                Q[q].wait_ge(T.sem[s], v)
+                seen[(q, s)] = v
+
+    V, S, P = g.vector, g.scalar, g.tensor
+    A = AluOpType
+    centre = [GAP + CAP + STR * i for i in range(NCH)]
+    lo = [c - CAP for c in centre]
+
+    wt = {}
+    if is_rank:
+        for i in range(8):
+            (g.sync if i % 2 == 0 else g.scalar).dma_start(T.E[16 * i:16 * i + 16, :], T.ex[:, :]).then_inc(T.sem.lde, 16)
+        t_ex = ("lde", 128)
+        b = side * 1024
+        g.sync.dma_start(T.w[:, b:b + 512], T.w1[:, :]).then_inc(T.sem["w1%d" % side], 16)
+        g.scalar.dma_start(T.xs[:, :], T.x[:, :]).then_inc(T.sem.ldx, 16)
+        g.scalar.dma_start(T.w[:, b + 512:b + 1024], T.w2[:, :]).then_inc(T.sem["w2%d" % side], 16)
+        t_x = ("ldx", 16)
+        total["lde"], total["ldx"] = 128, 16
+        wt[(1, side)] = ("w1%d" % side, 16)
+        wt[(2, side)] = ("w2%d" % side, 16)
+
+    peer = on[j][1 - side]
+    far = lane[((j + 1) % NCH, die)]
+    m_on = topo.mask(core, peer if is_rank else owner)
+    m_off = topo.mask(core, far)
+    m_hi = m_on & ~m_off
+    for e in range(2):
+        if (1, e) not in wt:
+            wt[(1, e)] = ("w1%d" % e, _bits(m_on))
+            wt[(2, e)] = ("w2%d" % e, _bits(m_hi))
+    for k in wt:
+        total[wt[k][0]] = wt[k][1]
+    sent = [0]
+
+    if is_rank:
+        t_p = done("g", g.iota(T.pcol[:, :], [[0, 1]], 0, 1))
+        t_gf = done("g", g.iota(T.gfree[:, :], [[1, 8], [0, 16]], 0, 0, allow_small_or_imprecise_dtypes=True))
+        t_vf = done("g", g.iota(T.vfree[:, :], [[32, 4], [15, 2], [1, 16]], 1, -1, allow_small_or_imprecise_dtypes=True))
+        t_af = done("g", g.iota(T.afree[:, :], [[0, 8], [1, 16]], 0, 0, allow_small_or_imprecise_dtypes=True))
+
+        done("v", V.memset(T.oh[:, :], 0.0))
+        done("v", V.memset(T.mask[:, :], 1.0))
+        need("v", t_p)
+        done("v", V.tensor_scalar(out=T.icol[:, 0:1], in0=T.pcol[:, :], scalar1=4, scalar2=None, op0=A.arith_shift_right))
+        done("v", V.tensor_scalar(out=T.icol[:, 1:2], in0=T.pcol[:, :], scalar1=4, scalar2=1,
+                                  op0=A.arith_shift_right, op1=A.bitwise_and))
+        done("v", V.tensor_scalar(out=T.icol[:, 2:3], in0=T.pcol[:, :], scalar1=5, scalar2=None, op0=A.arith_shift_right))
+        t_i = done("v", V.tensor_scalar(out=T.icol[:, 3:4], in0=T.pcol[:, :], scalar1=15, scalar2=None, op0=A.bitwise_and))
+        need("v", t_i)
+        done("v", V.tensor_copy(out=T.cols[:, 0:1], in_=T.icol[:, 0:1]))
+        done("v", V.tensor_scalar(out=T.cols[:, 1:2], in0=T.icol[:, 0:1], scalar1=8.0, scalar2=None, op0=A.add))
+        done("v", V.tensor_scalar(out=T.cols[:, 2:3], in0=T.icol[:, 1:2], scalar1=2.0, scalar2=-1.0,
+                                  op0=A.mult, op1=A.add))
+        done("v", V.tensor_scalar(out=T.cols[:, 3:4], in0=T.icol[:, 2:3], scalar1=float(STR), scalar2=float(centre[0]),
+                                  op0=A.mult, op1=A.add))
+        done("v", V.tensor_scalar(out=T.cols[:, 4:5], in0=T.icol[:, 2:3], scalar1=float(STR),
+                                  scalar2=float(centre[0] + 4 * STR), op0=A.mult, op1=A.add))
+        t_c = done("v", V.tensor_copy(out=T.cols[:, 5:6], in_=T.icol[:, 3:4]))
+        need("v", t_c, t_gf)
+        t_blk = done("v", V.tensor_scalar(out=T.blk[:, :], in0=T.gfree[:, :], scalar1=T.cols[:, 0:1],
+                                          scalar2=T.cols[:, 2:3], op0=A.is_equal, op1=A.mult))
+        need("v", t_vf)
+        t_pos = done("v", V.tensor_scalar(out=T.pos[:, :], in0=T.vfree[:, :], scalar1=0.0, scalar2=None, op0=A.is_gt))
+        need("v", t_pos)
+        t_tri = done("v", V.tensor_tensor(out=T.tri[:, :], in0=T.blk[:, :], in1=T.pos[:, :], op=A.mult))
+        need("v", t_tri)
+        t_rest = done("v", V.tensor_tensor(out=T.rest[:, :], in0=T.blk[:, :], in1=T.tri[:, :], op=A.subtract))
+        t_m = done("v", V.memset(T.mask[:, 17:18], 0.0))
+        need("v", t_af)
+        t_sel = done("v", V.tensor_scalar(out=T.sel[:, :], in0=T.afree[:, :], scalar1=T.cols[:, 5:6], scalar2=None,
+                                          op0=A.is_equal))
+        for i in range(NCH):
+            t_z = done("v", V.memset(T.send[:, lo[i]:lo[i] + BLK], 0.0))
+
+        need("v", t_ex)
+        done("v", V.tensor_scalar(out=T.oh[:, 1:17], in0=T.E[:, :], scalar1=T.cols[:, 0:1], scalar2=None, op0=A.is_equal))
+        t_oh = done("v", V.tensor_scalar(out=T.oh[:, 18:34], in0=T.E[:, :], scalar1=T.cols[:, 1:2], scalar2=None,
+                                         op0=A.is_equal))
+        need("p", t_oh)
+        done("p", P.matmul(T.pd[:, 0:33], T.rest[:, :], T.oh[:, 0:33], True, False))
+        t_d = done("p", P.matmul(T.pd[:, 0:33], T.tri[:, :], T.oh[:, 1:34], False, True))
+        need("s", t_oh)
+        done("s", S.activation(out=T.ohb[:, 0:16], in_=T.oh[:, 1:17], func=ActivationFunctionType.Identity,
+                               scale=T.cols[:, 3:4]))
+        t_ohb = done("s", S.activation(out=T.ohb[:, 16:32], in_=T.oh[:, 18:34], func=ActivationFunctionType.Identity,
+                                       scale=T.cols[:, 4:5]))
+        need("p", t_ohb)
+        done("p", P.matmul(T.po[:, 0:16], T.sel[:, :], T.ohb[:, 0:16], True, False))
+        done("p", P.matmul(T.po[:, 0:16], T.sel[:, :], T.ohb[:, 16:32], False, False))
+        need("v", t_d)
+        t_w = done("v", V.tensor_tensor_scan(out=T.wsc[:, 0:33], data0=T.mask[:, 0:33], data1=T.pd[:, 0:33], initial=0.0,
+                                             op0=A.mult, op1=A.add))
+        need("v", t_w)
+        t_v = done("v", V.tensor_tensor(out=T.val[:, 0:33], in0=T.oh[:, 1:34], in1=T.wsc[:, 0:33], op=A.mult))
+        need("p", t_v)
+        done("p", P.matmul(T.po[:, 0:16], T.sel[:, :], T.val[:, 0:16], False, False))
+        t_o = done("p", P.matmul(T.po[:, 0:16], T.sel[:, :], T.val[:, 17:33], False, True))
+        need("v", t_o)
+        t_off = done("v", V.tensor_copy(out=T.off[:, :], in_=T.po[:, 0:16]))
+        need("v", t_off, t_x)
+        t_sc = done("v", V.tensor_copy(out=T.send[:, 0:WIN].indirect(T.off[:, 0:16]), in_=T.xs[:, :]))
+        for i in range(NCH + 1):
+            t_gap = done("v", V.memset(T.ret[:, STR * i:STR * i + GAP], 0.0))
+
+        dsts = [peer] + ([helper[owner], helper[peer]] if HELPERS else [])
+        ids = [DstId(rid=topo.addr(d)[0], pnc=topo.addr(d)[1]) for d in dsts]
+        for layer, m in ((1, m_on), (2, m_hi)):
+            need("g", wt[(layer, side)])
+            piece = T.w[:, side * 1024 + (layer - 1) * 512:side * 1024 + layer * 512]
+            g.remote_dma_fused([RemoteDMATransfer(dst_ids=ids, dma_engine_mask=m, remote_sem=T.sem["w%d%d" % (layer, side)],
+                                                  srcs=[piece], dsts=[piece for d in dsts])], local_sem=T.sem.sent)
+            sent[0] += _bits(m)
+
+        need("g", t_sc)
+        for s in range(1, NCH):
+            i = (j + s) % NCH
+            d = worker(i, s)
+            rid, pid, _ = topo.addr(d)
+            m = topo.mask(core, d)
+            g.remote_dma(T.land[:, BLK * (s - 1):BLK * s], T.send[:, lo[i]:lo[i] + BLK], T.sem["ar%d" % s], T.sem.sent,
+                         pid, rid, m)
+            sent[0] += _bits(m)
+
+    PH = [[T.ph00, T.ph01], [T.ph10, T.ph11]]
+    PY = [T.py0, T.py1]
+    hist = []
+    order = [side, 1 - side]
+
+    def ffn(n, x, x0, t_in, out):
+        bb = n % 2
+        old = hist[n - 2] if n >= 2 else None
+        t1, tr, t2 = {}, {}, {}
+        for e in order:
+            need("p", t_in, wt[(1, e)])
+            for f in range(FF):
+                c0 = e * 1024 + f * 128
+                t1[e] = done("p", P.matmul(PH[bb][e][:, CAP * f:CAP * f + CAP], T.w[:, c0:c0 + 128],
+                                           x[:, x0 + CAP * e:x0 + CAP * e + CAP], True, True))
+        for e in order:
+            h = T.hs[:, (2 * bb + e) * 192:(2 * bb + e) * 192 + 192]
+            q = "v" if e == order[0] else "s"
+            need(q, t1[e], old[0][e] if old else None)
+            if q == "v":
+                tr[e] = done("v", V.tensor_scalar(out=h, in0=PH[bb][e][:, 0:192], scalar1=0.0, scalar2=None, op0=A.max))
+            else:
+                tr[e] = done("s", S.activation(out=h, in_=PH[bb][e][:, 0:192], func=ActivationFunctionType.Relu))
+        for e in order:
+            need("p", tr[e], wt[(2, e)], old[1] if old else None)
+            for f in range(FF):
+                c0 = e * 1024 + 512 + f * 128
+                h0 = (2 * bb + e) * 192 + CAP * f
+                t2[e] = done("p", P.matmul(PY[bb][:, CAP * e:CAP * e + CAP], T.w[:, c0:c0 + 128], T.hs[:, h0:h0 + CAP],
+                                           f == 0, f == FF - 1))
+        need("v", t2[order[1]])
+        t_out = done("v", V.tensor_copy(out=out, in_=PY[bb][:, 0:BLK]))
+        hist.append((t2, t_out))
+        return t_out
+
+    n = 0
+    t_own = None
+    if is_rank:
+        t_own = ffn(n, T.send, lo[j], t_sc, T.ret[:, lo[j]:lo[j] + BLK])
+        n += 1
+    for s in my_rounds:
+        total["ar%d" % s] = _bits(m_off)
+        t_res = ffn(n, T.land, BLK * (s - 1), ("ar%d" % s, _bits(m_off)), T.outb[:, BLK * (s - 1):BLK * s])
+        n += 1
+        src = lane[((j - s) % NCH, die)]
+        rid, pid, _ = topo.addr(src)
+        m = topo.mask(core, src)
+        need("g", t_res)
+        g.remote_dma(T.ret[:, lo[j]:lo[j] + BLK], T.outb[:, BLK * (s - 1):BLK * s], T.sem.back, T.sem.sent, pid, rid, m)
+        sent[0] += _bits(m)
+
+    if is_rank:
+        t_back = ("back", (NCH - 1) * _bits(m_off))
+        total["back"] = t_back[1]
+        half = TOK // 2
+        need("v", t_back, t_own, t_gap)
+        t_y0 = done("v", V.tensor_copy(out=T.ysb[:, 0:half], in_=T.ret[:, 0:WIN].indirect(T.off[:, 0:8])))
+        need("s", t_back, t_own, t_gap)
+        t_y1 = done("s", S.activation(out=T.ysb[:, half:TOK], in_=T.ret[:, 0:WIN].indirect(T.off[:, 8:16]),
+                                      func=ActivationFunctionType.Copy))
+        need("y", t_y0)
+        g.sync.dma_start(T.y[:, 0:half], T.ysb[:, 0:half]).then_inc(T.sem.st, 16)
+        need("s", t_y1)
+        g.scalar.dma_start(T.y[:, half:TOK], T.ysb[:, half:TOK]).then_inc(T.sem.st, 16)
+        total["st"] = 32
+
+    total["sent"] = sent[0]
+    for s in SEMAPHORES:
+        if total.get(s, 0) > 0:
+            need("g", (s, total[s]))

@@ -2,7 +2,6 @@ import numpy as np
 from concourse.bass import DstId, RemoteDMATransfer
 from concourse.mybir import AluOpType, ActivationFunctionType
 
-HELPERS = True
 CAP, TOK, FF = 48, 256, 4
 BLK = 2 * CAP
 GAP = TOK - CAP
@@ -23,17 +22,20 @@ SCRATCH = {
     "off": ("sbuf", [128, 16], "uint16"),
     "pcol": ("sbuf", [128, 1], "int32"),
     "icol": ("sbuf", [128, 4], "int32"),
-    "cols": ("sbuf", [128, 8], "float32"),
-    "gfree": ("sbuf", [128, 128], "bfloat16"),
+    "fcol": ("sbuf", [128, 4], "float32"),
+    "cols": ("sbuf", [128, 4], "float32"),
+    "bcol": ("sbuf", [128, 4], "float32"),
     "vfree": ("sbuf", [128, 128], "bfloat16"),
+    "mfree": ("sbuf", [128, 128], "bfloat16"),
     "afree": ("sbuf", [128, 128], "bfloat16"),
-    "blk": ("sbuf", [128, 128], "bfloat16"),
-    "pos": ("sbuf", [128, 128], "bfloat16"),
-    "tri": ("sbuf", [128, 128], "bfloat16"),
-    "rest": ("sbuf", [128, 128], "bfloat16"),
+    "ml": ("sbuf", [128, 128], "bfloat16"),
+    "mnl": ("sbuf", [128, 128], "bfloat16"),
+    "mn2": ("sbuf", [128, 128], "bfloat16"),
+    "m3": ("sbuf", [128, 128], "bfloat16"),
     "sel": ("sbuf", [128, 128], "bfloat16"),
     "mask": ("sbuf", [128, 40], "float32"),
     "oh": ("sbuf", [128, 40], "bfloat16"),
+    "oha": ("sbuf", [128, 40], "bfloat16"),
     "ohb": ("sbuf", [128, 32], "bfloat16"),
     "wsc": ("sbuf", [128, 40], "float32"),
     "val": ("sbuf", [128, 40], "bfloat16"),
@@ -70,17 +72,16 @@ def _plan(T, topo):
         for c in on[j]:
             lane[(j, topo.die(c))] = c
     helper = {}
-    if HELPERS:
-        for j in range(NCH):
-            for c in on[j]:
-                d = topo.die(c)
-                for h in range(min(on[j]) - 8, max(on[j]) + 8):
-                    if h < 0 or h in cores or topo.chip(h) != chips[j] or topo.die(h) != d:
-                        continue
-                    if all(topo.may_write(h, lane[(i, d)]) for i in range(NCH) if i != j):
-                        helper[c] = h
-                        break
-                assert c in helper
+    for j in range(NCH):
+        for c in on[j]:
+            d = topo.die(c)
+            for h in range(min(on[j]) - 8, max(on[j]) + 8):
+                if h < 0 or h in cores or topo.chip(h) != chips[j] or topo.die(h) != d:
+                    continue
+                if all(topo.may_write(h, lane[(i, d)]) for i in range(NCH) if i != j):
+                    helper[c] = h
+                    break
+            assert c in helper
     return cores, chips, on, lane, helper
 
 
@@ -99,7 +100,7 @@ def rank_program(g, core, T, topo):
 
     def worker(ch, s):
         r = lane[(ch, die)]
-        return helper[r] if (HELPERS and s % 2 == 1) else r
+        return helper[r] if s % 2 == 1 else r
 
     my_rounds = [s for s in range(1, NCH) if worker(j, s) == core]
 
@@ -126,8 +127,14 @@ def rank_program(g, core, T, topo):
 
     V, S, P = g.vector, g.scalar, g.tensor
     A = AluOpType
+    F = ActivationFunctionType
     centre = [GAP + CAP + STR * i for i in range(NCH)]
     lo = [c - CAP for c in centre]
+
+    def ts(out, in0, s1, op0, s2=None, op1=None):
+        if op1 is None:
+            return done("v", V.tensor_scalar(out=out, in0=in0, scalar1=s1, scalar2=None, op0=op0))
+        return done("v", V.tensor_scalar(out=out, in0=in0, scalar1=s1, scalar2=s2, op0=op0, op1=op1))
 
     wt = {}
     if is_rank:
@@ -148,6 +155,7 @@ def rank_program(g, core, T, topo):
     m_on = topo.mask(core, peer if is_rank else owner)
     m_off = topo.mask(core, far)
     m_hi = m_on & ~m_off
+    n_off = _bits(m_off)
     for e in range(2):
         if (1, e) not in wt:
             wt[(1, e)] = ("w1%d" % e, _bits(m_on))
@@ -156,77 +164,80 @@ def rank_program(g, core, T, topo):
         total[wt[k][0]] = wt[k][1]
     sent = [0]
 
+    def write(dst, out, in_, sem):
+        rid, pid, _ = topo.addr(dst)
+        m = topo.mask(core, dst)
+        g.remote_dma(out, in_, sem, T.sem.sent, pid, rid, m)
+        sent[0] += _bits(m)
+
     if is_rank:
         t_p = done("g", g.iota(T.pcol[:, :], [[0, 1]], 0, 1))
-        t_gf = done("g", g.iota(T.gfree[:, :], [[1, 8], [0, 16]], 0, 0, allow_small_or_imprecise_dtypes=True))
         t_vf = done("g", g.iota(T.vfree[:, :], [[32, 4], [15, 2], [1, 16]], 1, -1, allow_small_or_imprecise_dtypes=True))
+        t_mf = done("g", g.iota(T.mfree[:, :], [[16, 8], [0, 16]], 0, -1, allow_small_or_imprecise_dtypes=True))
         t_af = done("g", g.iota(T.afree[:, :], [[0, 8], [1, 16]], 0, 0, allow_small_or_imprecise_dtypes=True))
 
         done("v", V.memset(T.oh[:, :], 0.0))
-        done("v", V.memset(T.mask[:, :], 1.0))
+        done("v", V.memset(T.oha[:, :], 0.0))
+        need("v", done("v", V.memset(T.mask[:, :], 1.0)))
+        done("v", V.memset(T.mask[:, 17:18], 0.0))
         need("v", t_p)
-        done("v", V.tensor_scalar(out=T.icol[:, 0:1], in0=T.pcol[:, :], scalar1=4, scalar2=None, op0=A.arith_shift_right))
-        done("v", V.tensor_scalar(out=T.icol[:, 1:2], in0=T.pcol[:, :], scalar1=4, scalar2=1,
-                                  op0=A.arith_shift_right, op1=A.bitwise_and))
-        done("v", V.tensor_scalar(out=T.icol[:, 2:3], in0=T.pcol[:, :], scalar1=5, scalar2=None, op0=A.arith_shift_right))
-        t_i = done("v", V.tensor_scalar(out=T.icol[:, 3:4], in0=T.pcol[:, :], scalar1=15, scalar2=None, op0=A.bitwise_and))
-        need("v", t_i)
-        done("v", V.tensor_copy(out=T.cols[:, 0:1], in_=T.icol[:, 0:1]))
-        done("v", V.tensor_scalar(out=T.cols[:, 1:2], in0=T.icol[:, 0:1], scalar1=8.0, scalar2=None, op0=A.add))
-        done("v", V.tensor_scalar(out=T.cols[:, 2:3], in0=T.icol[:, 1:2], scalar1=2.0, scalar2=-1.0,
-                                  op0=A.mult, op1=A.add))
-        done("v", V.tensor_scalar(out=T.cols[:, 3:4], in0=T.icol[:, 2:3], scalar1=float(STR), scalar2=float(centre[0]),
-                                  op0=A.mult, op1=A.add))
-        done("v", V.tensor_scalar(out=T.cols[:, 4:5], in0=T.icol[:, 2:3], scalar1=float(STR),
-                                  scalar2=float(centre[0] + 4 * STR), op0=A.mult, op1=A.add))
-        t_c = done("v", V.tensor_copy(out=T.cols[:, 5:6], in_=T.icol[:, 3:4]))
-        need("v", t_c, t_gf)
-        t_blk = done("v", V.tensor_scalar(out=T.blk[:, :], in0=T.gfree[:, :], scalar1=T.cols[:, 0:1],
-                                          scalar2=T.cols[:, 2:3], op0=A.is_equal, op1=A.mult))
+        ts(T.icol[:, 0:1], T.pcol[:, :], 4, A.arith_shift_right)
+        ts(T.icol[:, 1:2], T.pcol[:, :], 4, A.arith_shift_right, 1, A.bitwise_and)
+        ts(T.icol[:, 2:3], T.pcol[:, :], 5, A.arith_shift_right)
+        need("v", ts(T.icol[:, 3:4], T.pcol[:, :], 15, A.bitwise_and))
+        t_f = done("v", V.tensor_copy(out=T.fcol[:, :], in_=T.icol[:, :]))
+        need("v", t_f)
+        ts(T.cols[:, 0:1], T.fcol[:, 0:1], 8.0, A.add)
+        ts(T.cols[:, 1:2], T.fcol[:, 1:2], 2.0, A.mult, -1.0, A.add)
         need("v", t_vf)
-        t_pos = done("v", V.tensor_scalar(out=T.pos[:, :], in0=T.vfree[:, :], scalar1=0.0, scalar2=None, op0=A.is_gt))
-        need("v", t_pos)
-        t_tri = done("v", V.tensor_tensor(out=T.tri[:, :], in0=T.blk[:, :], in1=T.pos[:, :], op=A.mult))
-        need("v", t_tri)
-        t_rest = done("v", V.tensor_tensor(out=T.rest[:, :], in0=T.blk[:, :], in1=T.tri[:, :], op=A.subtract))
-        t_m = done("v", V.memset(T.mask[:, 17:18], 0.0))
-        need("v", t_af)
-        t_sel = done("v", V.tensor_scalar(out=T.sel[:, :], in0=T.afree[:, :], scalar1=T.cols[:, 5:6], scalar2=None,
-                                          op0=A.is_equal))
-        for i in range(NCH):
-            t_z = done("v", V.memset(T.send[:, lo[i]:lo[i] + BLK], 0.0))
+        ts(T.ml[:, :], T.vfree[:, :], 0.0, A.is_gt)
+        ts(T.mnl[:, :], T.vfree[:, :], 0.0, A.is_gt, -1.0, A.mult)
+        need("v", t_mf)
+        ts(T.mn2[:, :], T.mfree[:, :], 0.0, A.is_gt, -1.0, A.mult)
+        t_m3 = ts(T.m3[:, :], T.mfree[:, :], -16.0, A.is_gt)
 
-        need("v", t_ex)
-        done("v", V.tensor_scalar(out=T.oh[:, 1:17], in0=T.E[:, :], scalar1=T.cols[:, 0:1], scalar2=None, op0=A.is_equal))
-        t_oh = done("v", V.tensor_scalar(out=T.oh[:, 18:34], in0=T.E[:, :], scalar1=T.cols[:, 1:2], scalar2=None,
-                                         op0=A.is_equal))
+        need("s", t_f)
+        done("s", S.activation(out=T.bcol[:, 0:1], in_=T.fcol[:, 2:3], func=F.Identity, bias=float(centre[0]),
+                               scale=float(STR)))
+        t_b = done("s", S.activation(out=T.bcol[:, 1:2], in_=T.fcol[:, 2:3], func=F.Identity, bias=float(centre[4]),
+                                     scale=float(STR)))
+        need("s", t_vf)
+        for i in range(3):
+            t_z = done("s", S.activation(out=T.send[:, lo[i]:lo[i] + BLK], in_=T.vfree[:, 0:BLK], func=F.Copy, scale=0.0))
+
+        need("v", t_m3, t_ex)
+        ts(T.oh[:, 1:17], T.E[:, :], T.fcol[:, 0:1], A.is_equal)
+        t_oh = ts(T.oh[:, 18:34], T.E[:, :], T.cols[:, 0:1], A.is_equal)
         need("p", t_oh)
-        done("p", P.matmul(T.pd[:, 0:33], T.rest[:, :], T.oh[:, 0:33], True, False))
-        t_d = done("p", P.matmul(T.pd[:, 0:33], T.tri[:, :], T.oh[:, 1:34], False, True))
-        need("s", t_oh)
-        done("s", S.activation(out=T.ohb[:, 0:16], in_=T.oh[:, 1:17], func=ActivationFunctionType.Identity,
-                               scale=T.cols[:, 3:4]))
-        t_ohb = done("s", S.activation(out=T.ohb[:, 16:32], in_=T.oh[:, 18:34], func=ActivationFunctionType.Identity,
-                                       scale=T.cols[:, 4:5]))
-        need("p", t_ohb)
+        done("p", P.matmul(T.pd[:, 0:33], T.m3[:, :], T.oh[:, 0:33], True, False))
+        done("p", P.matmul(T.pd[:, 0:33], T.mnl[:, :], T.oh[:, 0:33], False, False))
+        done("p", P.matmul(T.pd[:, 0:33], T.ml[:, :], T.oh[:, 1:34], False, False))
+        t_d = done("p", P.matmul(T.pd[:, 0:33], T.mn2[:, :], T.oh[:, 1:34], False, True))
+        need("s", t_oh, t_b)
+        done("s", S.activation(out=T.ohb[:, 0:16], in_=T.oh[:, 1:17], func=F.Identity, scale=T.bcol[:, 0:1]))
+        t_ohb = done("s", S.activation(out=T.ohb[:, 16:32], in_=T.oh[:, 18:34], func=F.Identity, scale=T.bcol[:, 1:2]))
+        ts(T.oha[:, 1:17], T.E[:, :], T.fcol[:, 0:1], A.is_equal, T.cols[:, 1:2], A.mult)
+        ts(T.oha[:, 18:34], T.E[:, :], T.cols[:, 0:1], A.is_equal, T.cols[:, 1:2], A.mult)
+        need("v", t_af)
+        t_sel = ts(T.sel[:, :], T.afree[:, :], T.fcol[:, 3:4], A.is_equal)
+        need("p", t_ohb, t_sel)
         done("p", P.matmul(T.po[:, 0:16], T.sel[:, :], T.ohb[:, 0:16], True, False))
         done("p", P.matmul(T.po[:, 0:16], T.sel[:, :], T.ohb[:, 16:32], False, False))
         need("v", t_d)
-        t_w = done("v", V.tensor_tensor_scan(out=T.wsc[:, 0:33], data0=T.mask[:, 0:33], data1=T.pd[:, 0:33], initial=0.0,
-                                             op0=A.mult, op1=A.add))
-        need("v", t_w)
-        t_v = done("v", V.tensor_tensor(out=T.val[:, 0:33], in0=T.oh[:, 1:34], in1=T.wsc[:, 0:33], op=A.mult))
-        need("p", t_v)
+        need("v", done("v", V.tensor_tensor_scan(out=T.wsc[:, 0:33], data0=T.mask[:, 0:33], data1=T.pd[:, 0:33],
+                                                 initial=0.0, op0=A.mult, op1=A.add)))
+        need("p", done("v", V.tensor_tensor(out=T.val[:, 0:33], in0=T.oha[:, 1:34], in1=T.wsc[:, 0:33], op=A.mult)))
         done("p", P.matmul(T.po[:, 0:16], T.sel[:, :], T.val[:, 0:16], False, False))
         t_o = done("p", P.matmul(T.po[:, 0:16], T.sel[:, :], T.val[:, 17:33], False, True))
+        for i in range(3, NCH):
+            done("v", V.memset(T.send[:, lo[i]:lo[i] + BLK], 0.0))
         need("v", t_o)
-        t_off = done("v", V.tensor_copy(out=T.off[:, :], in_=T.po[:, 0:16]))
-        need("v", t_off, t_x)
+        need("v", done("v", V.tensor_copy(out=T.off[:, :], in_=T.po[:, 0:16])), t_x, t_z)
         t_sc = done("v", V.tensor_copy(out=T.send[:, 0:WIN].indirect(T.off[:, 0:16]), in_=T.xs[:, :]))
         for i in range(NCH + 1):
             t_gap = done("v", V.memset(T.ret[:, STR * i:STR * i + GAP], 0.0))
 
-        dsts = [peer] + ([helper[owner], helper[peer]] if HELPERS else [])
+        dsts = [peer, helper[owner], helper[peer]]
         ids = [DstId(rid=topo.addr(d)[0], pnc=topo.addr(d)[1]) for d in dsts]
         for layer, m in ((1, m_on), (2, m_hi)):
             need("g", wt[(layer, side)])
@@ -238,12 +249,7 @@ def rank_program(g, core, T, topo):
         need("g", t_sc)
         for s in range(1, NCH):
             i = (j + s) % NCH
-            d = worker(i, s)
-            rid, pid, _ = topo.addr(d)
-            m = topo.mask(core, d)
-            g.remote_dma(T.land[:, BLK * (s - 1):BLK * s], T.send[:, lo[i]:lo[i] + BLK], T.sem["ar%d" % s], T.sem.sent,
-                         pid, rid, m)
-            sent[0] += _bits(m)
+            write(worker(i, s), T.land[:, BLK * (s - 1):BLK * s], T.send[:, lo[i]:lo[i] + BLK], T.sem["ar%d" % s])
 
     PH = [[T.ph00, T.ph01], [T.ph10, T.ph11]]
     PY = [T.py0, T.py1]
@@ -265,9 +271,9 @@ def rank_program(g, core, T, topo):
             q = "v" if e == order[0] else "s"
             need(q, t1[e], old[0][e] if old else None)
             if q == "v":
-                tr[e] = done("v", V.tensor_scalar(out=h, in0=PH[bb][e][:, 0:192], scalar1=0.0, scalar2=None, op0=A.max))
+                tr[e] = ts(h, PH[bb][e][:, 0:192], 0.0, A.max)
             else:
-                tr[e] = done("s", S.activation(out=h, in_=PH[bb][e][:, 0:192], func=ActivationFunctionType.Relu))
+                tr[e] = done("s", S.activation(out=h, in_=PH[bb][e][:, 0:192], func=F.Relu))
         for e in order:
             need("p", tr[e], wt[(2, e)], old[1] if old else None)
             for f in range(FF):
@@ -281,30 +287,24 @@ def rank_program(g, core, T, topo):
         return t_out
 
     n = 0
-    t_own = None
     if is_rank:
         t_own = ffn(n, T.send, lo[j], t_sc, T.ret[:, lo[j]:lo[j] + BLK])
         n += 1
     for s in my_rounds:
-        total["ar%d" % s] = _bits(m_off)
-        t_res = ffn(n, T.land, BLK * (s - 1), ("ar%d" % s, _bits(m_off)), T.outb[:, BLK * (s - 1):BLK * s])
+        total["ar%d" % s] = n_off
+        o0 = BLK * (s - 1)
+        need("g", ffn(n, T.land, o0, ("ar%d" % s, n_off), T.outb[:, o0:o0 + BLK]))
+        write(lane[((j - s) % NCH, die)], T.ret[:, lo[j]:lo[j] + BLK], T.outb[:, o0:o0 + BLK], T.sem.back)
         n += 1
-        src = lane[((j - s) % NCH, die)]
-        rid, pid, _ = topo.addr(src)
-        m = topo.mask(core, src)
-        need("g", t_res)
-        g.remote_dma(T.ret[:, lo[j]:lo[j] + BLK], T.outb[:, BLK * (s - 1):BLK * s], T.sem.back, T.sem.sent, pid, rid, m)
-        sent[0] += _bits(m)
 
     if is_rank:
-        t_back = ("back", (NCH - 1) * _bits(m_off))
+        t_back = ("back", (NCH - 1) * n_off)
         total["back"] = t_back[1]
         half = TOK // 2
         need("v", t_back, t_own, t_gap)
         t_y0 = done("v", V.tensor_copy(out=T.ysb[:, 0:half], in_=T.ret[:, 0:WIN].indirect(T.off[:, 0:8])))
         need("s", t_back, t_own, t_gap)
-        t_y1 = done("s", S.activation(out=T.ysb[:, half:TOK], in_=T.ret[:, 0:WIN].indirect(T.off[:, 8:16]),
-                                      func=ActivationFunctionType.Copy))
+        t_y1 = done("s", S.activation(out=T.ysb[:, half:TOK], in_=T.ret[:, 0:WIN].indirect(T.off[:, 8:16]), func=F.Copy))
         need("y", t_y0)
         g.sync.dma_start(T.y[:, 0:half], T.ysb[:, 0:half]).then_inc(T.sem.st, 16)
         need("s", t_y1)

import numpy as np
from concourse.bass import DstId, RemoteDMATransfer
from concourse.mybir import AluOpType, ActivationFunctionType

CAP, TOK, FF = 48, 256, 4
BLK = 2 * CAP
GAP = TOK - CAP
STR = BLK + GAP
NCH = 5
WIN = GAP + NCH * STR

SCRATCH = {
    "E": ("sbuf", [128, 16], "int32"),
    "xs": ("sbuf", [128, TOK], "bfloat16"),
    "w": ("sbuf", [128, 2048], "bfloat16"),
    "send": ("sbuf", [128, WIN], "bfloat16"),
    "ret": ("sbuf", [128, WIN], "bfloat16"),
    "land": ("sbuf", [128, 4 * BLK], "bfloat16"),
    "outb": ("sbuf", [128, 4 * BLK], "bfloat16"),
    "hs": ("sbuf", [128, 4 * 192], "bfloat16"),
    "ysb": ("sbuf", [128, TOK], "bfloat16"),
    "off": ("sbuf", [128, 16], "uint16"),
    "pcol": ("sbuf", [128, 1], "int32"),
    "icol": ("sbuf", [128, 4], "int32"),
    "fcol": ("sbuf", [128, 4], "float32"),
    "cols": ("sbuf", [128, 4], "float32"),
    "bcol": ("sbuf", [128, 4], "float32"),
    "vfree": ("sbuf", [128, 128], "bfloat16"),
    "mfree": ("sbuf", [128, 128], "bfloat16"),
    "afree": ("sbuf", [128, 128], "bfloat16"),
    "ml": ("sbuf", [128, 128], "bfloat16"),
    "mnl": ("sbuf", [128, 128], "bfloat16"),
    "mn2": ("sbuf", [128, 128], "bfloat16"),
    "m3": ("sbuf", [128, 128], "bfloat16"),
    "sel": ("sbuf", [128, 128], "bfloat16"),
    "mask": ("sbuf", [128, 40], "float32"),
    "oh": ("sbuf", [128, 40], "bfloat16"),
    "oha": ("sbuf", [128, 40], "bfloat16"),
    "ohb": ("sbuf", [128, 32], "bfloat16"),
    "wsc": ("sbuf", [128, 40], "float32"),
    "val": ("sbuf", [128, 40], "bfloat16"),
    "pd": ("psum", [128, 512], "float32"),
    "po": ("psum", [128, 512], "float32"),
    "ph00": ("psum", [128, 512], "float32"),
    "ph01": ("psum", [128, 512], "float32"),
    "ph10": ("psum", [128, 512], "float32"),
    "ph11": ("psum", [128, 512], "float32"),
    "py0": ("psum", [128, 512], "float32"),
    "py1": ("psum", [128, 512], "float32"),
}
SEMAPHORES = ["cv", "cs", "cp", "cg", "lde", "ldx", "w10", "w11", "w20", "w21",
              "ar1", "ar2", "ar3", "ar4", "back", "sent", "st"]


def _bits(m):
    return bin(m).count("1")


def _plan(T, topo):
    cores = list(T.cores)
    chips = []
    for c in cores:
        if topo.chip(c) not in chips:
            chips.append(topo.chip(c))
    assert len(chips) == NCH
    on = [[c for c in cores if topo.chip(c) == ch] for ch in chips]
    for j in range(NCH):
        assert len(on[j]) == 2 and cores.index(on[j][0]) == 2 * j and cores.index(on[j][1]) == 2 * j + 1
        assert topo.die(on[j][0]) != topo.die(on[j][1])
    lane = {}
    for j in range(NCH):
        for c in on[j]:
            lane[(j, topo.die(c))] = c
    helper = {}
    for j in range(NCH):
        for c in on[j]:
            d = topo.die(c)
            for h in range(min(on[j]) - 8, max(on[j]) + 8):
                if h < 0 or h in cores or topo.chip(h) != chips[j] or topo.die(h) != d:
                    continue
                if all(topo.may_write(h, lane[(i, d)]) for i in range(NCH) if i != j):
                    helper[c] = h
                    break
            assert c in helper
    return cores, chips, on, lane, helper


def rank_program(g, core, T, topo):
    cores, chips, on, lane, helper = _plan(T, topo)
    is_rank = core in cores
    owner = core if is_rank else None
    for c in helper:
        if helper[c] == core:
            owner = c
    if owner is None:
        return
    j = chips.index(topo.chip(core))
    die = topo.die(core)
    side = on[j].index(owner)

    def worker(ch, s):
        r = lane[(ch, die)]
        return helper[r] if s % 2 == 1 else r

    my_rounds = [s for s in range(1, NCH) if worker(j, s) == core]

    Q = {"v": g.vector, "s": g.scalar, "p": g.tensor, "g": g, "y": g.sync}
    cnt = {"cv": 0, "cs": 0, "cp": 0, "cg": 0}
    total = {}
    seen = {}

    def done(q, ins):
        s = "c" + q
        ins.then_inc(T.sem[s], 1)
        cnt[s] += 1
        total[s] = cnt[s]
        return (s, cnt[s])

    def need(q, *tickets):
        for t in tickets:
            if t is None:
                continue
            s, v = t
            if seen.get((q, s), 0) < v:
                Q[q].wait_ge(T.sem[s], v)
                seen[(q, s)] = v

    V, S, P = g.vector, g.scalar, g.tensor
    A = AluOpType
    F = ActivationFunctionType
    centre = [GAP + CAP + STR * i for i in range(NCH)]
    lo = [c - CAP for c in centre]

    def ts(out, in0, s1, op0, s2=None, op1=None):
        if op1 is None:
            return done("v", V.tensor_scalar(out=out, in0=in0, scalar1=s1, scalar2=None, op0=op0))
        return done("v", V.tensor_scalar(out=out, in0=in0, scalar1=s1, scalar2=s2, op0=op0, op1=op1))

    wt = {}
    if is_rank:
        for i in range(8):
            (g.sync if i % 2 == 0 else g.scalar).dma_start(T.E[16 * i:16 * i + 16, :], T.ex[:, :]).then_inc(T.sem.lde, 16)
        t_ex = ("lde", 128)
        b = side * 1024
        g.sync.dma_start(T.w[:, b:b + 512], T.w1[:, :]).then_inc(T.sem["w1%d" % side], 16)
        g.scalar.dma_start(T.xs[:, :], T.x[:, :]).then_inc(T.sem.ldx, 16)
        g.scalar.dma_start(T.w[:, b + 512:b + 1024], T.w2[:, :]).then_inc(T.sem["w2%d" % side], 16)
        t_x = ("ldx", 16)
        total["lde"], total["ldx"] = 128, 16
        wt[(1, side)] = ("w1%d" % side, 16)
        wt[(2, side)] = ("w2%d" % side, 16)

    peer = on[j][1 - side]
    far = lane[((j + 1) % NCH, die)]
    m_on = topo.mask(core, peer if is_rank else owner)
    m_off = topo.mask(core, far)
    m_hi = m_on & ~m_off
    n_off = _bits(m_off)
    for e in range(2):
        if (1, e) not in wt:
            wt[(1, e)] = ("w1%d" % e, _bits(m_on))
            wt[(2, e)] = ("w2%d" % e, _bits(m_hi))
    for k in wt:
        total[wt[k][0]] = wt[k][1]
    sent = [0]

    def write(dst, out, in_, sem):
        rid, pid, _ = topo.addr(dst)
        m = topo.mask(core, dst)
        g.remote_dma(out, in_, sem, T.sem.sent, pid, rid, m)
        sent[0] += _bits(m)

    if is_rank:
        t_p = done("g", g.iota(T.pcol[:, :], [[0, 1]], 0, 1))
        t_vf = done("g", g.iota(T.vfree[:, :], [[32, 4], [15, 2], [1, 16]], 1, -1, allow_small_or_imprecise_dtypes=True))
        t_mf = done("g", g.iota(T.mfree[:, :], [[16, 8], [0, 16]], 0, -1, allow_small_or_imprecise_dtypes=True))
        t_af = done("g", g.iota(T.afree[:, :], [[0, 8], [1, 16]], 0, 0, allow_small_or_imprecise_dtypes=True))

        done("v", V.memset(T.oh[:, :], 0.0))
        done("v", V.memset(T.oha[:, :], 0.0))
        need("v", done("v", V.memset(T.mask[:, :], 1.0)))
        done("v", V.memset(T.mask[:, 17:18], 0.0))
        need("v", t_p)
        ts(T.icol[:, 0:1], T.pcol[:, :], 4, A.arith_shift_right)
        ts(T.icol[:, 1:2], T.pcol[:, :], 4, A.arith_shift_right, 1, A.bitwise_and)
        ts(T.icol[:, 2:3], T.pcol[:, :], 5, A.arith_shift_right)
        need("v", ts(T.icol[:, 3:4], T.pcol[:, :], 15, A.bitwise_and))
        t_f = done("v", V.tensor_copy(out=T.fcol[:, :], in_=T.icol[:, :]))
        need("v", t_f)
        ts(T.cols[:, 0:1], T.fcol[:, 0:1], 8.0, A.add)
        ts(T.cols[:, 1:2], T.fcol[:, 1:2], 2.0, A.mult, -1.0, A.add)
        need("v", t_vf)
        ts(T.ml[:, :], T.vfree[:, :], 0.0, A.is_gt)
        ts(T.mnl[:, :], T.vfree[:, :], 0.0, A.is_gt, -1.0, A.mult)
        need("v", t_mf)
        ts(T.mn2[:, :], T.mfree[:, :], 0.0, A.is_gt, -1.0, A.mult)
        t_m3 = ts(T.m3[:, :], T.mfree[:, :], -16.0, A.is_gt)

        need("s", t_f)
        done("s", S.activation(out=T.bcol[:, 0:1], in_=T.fcol[:, 2:3], func=F.Identity, bias=float(centre[0]),
                               scale=float(STR)))
        t_b = done("s", S.activation(out=T.bcol[:, 1:2], in_=T.fcol[:, 2:3], func=F.Identity, bias=float(centre[4]),
                                     scale=float(STR)))
        need("s", t_vf)
        for i in range(3):
            t_z = done("s", S.activation(out=T.send[:, lo[i]:lo[i] + BLK], in_=T.vfree[:, 0:BLK], func=F.Copy, scale=0.0))

        need("v", t_m3, t_ex)
        ts(T.oh[:, 1:17], T.E[:, :], T.fcol[:, 0:1], A.is_equal)
        t_oh = ts(T.oh[:, 18:34], T.E[:, :], T.cols[:, 0:1], A.is_equal)
        need("p", t_oh)
        done("p", P.matmul(T.pd[:, 0:33], T.m3[:, :], T.oh[:, 0:33], True, False))
        done("p", P.matmul(T.pd[:, 0:33], T.mnl[:, :], T.oh[:, 0:33], False, False))
        done("p", P.matmul(T.pd[:, 0:33], T.ml[:, :], T.oh[:, 1:34], False, False))
        t_d = done("p", P.matmul(T.pd[:, 0:33], T.mn2[:, :], T.oh[:, 1:34], False, True))
        need("s", t_oh, t_b)
        done("s", S.activation(out=T.ohb[:, 0:16], in_=T.oh[:, 1:17], func=F.Identity, scale=T.bcol[:, 0:1]))
        t_ohb = done("s", S.activation(out=T.ohb[:, 16:32], in_=T.oh[:, 18:34], func=F.Identity, scale=T.bcol[:, 1:2]))
        ts(T.oha[:, 1:17], T.E[:, :], T.fcol[:, 0:1], A.is_equal, T.cols[:, 1:2], A.mult)
        ts(T.oha[:, 18:34], T.E[:, :], T.cols[:, 0:1], A.is_equal, T.cols[:, 1:2], A.mult)
        need("v", t_af)
        t_sel = ts(T.sel[:, :], T.afree[:, :], T.fcol[:, 3:4], A.is_equal)
        need("p", t_ohb, t_sel)
        done("p", P.matmul(T.po[:, 0:16], T.sel[:, :], T.ohb[:, 0:16], True, False))
        done("p", P.matmul(T.po[:, 0:16], T.sel[:, :], T.ohb[:, 16:32], False, False))
        need("v", t_d)
        need("v", done("v", V.tensor_tensor_scan(out=T.wsc[:, 0:33], data0=T.mask[:, 0:33], data1=T.pd[:, 0:33],
                                                 initial=0.0, op0=A.mult, op1=A.add)))
        need("p", done("v", V.tensor_tensor(out=T.val[:, 0:33], in0=T.oha[:, 1:34], in1=T.wsc[:, 0:33], op=A.mult)))
        done("p", P.matmul(T.po[:, 0:16], T.sel[:, :], T.val[:, 0:16], False, False))
        t_o = done("p", P.matmul(T.po[:, 0:16], T.sel[:, :], T.val[:, 17:33], False, True))
        for i in range(3, NCH):
            done("v", V.memset(T.send[:, lo[i]:lo[i] + BLK], 0.0))
        need("v", t_o)
        need("v", done("v", V.tensor_copy(out=T.off[:, :], in_=T.po[:, 0:16])), t_x, t_z)
        t_sc = done("v", V.tensor_copy(out=T.send[:, 0:WIN].indirect(T.off[:, 0:16]), in_=T.xs[:, :]))
        for i in range(NCH + 1):
            t_gap = done("v", V.memset(T.ret[:, STR * i:STR * i + GAP], 0.0))

        dsts = [peer, helper[owner], helper[peer]]
        ids = [DstId(rid=topo.addr(d)[0], pnc=topo.addr(d)[1]) for d in dsts]
        for layer, m in ((1, m_on), (2, m_hi)):
            need("g", wt[(layer, side)])
            piece = T.w[:, side * 1024 + (layer - 1) * 512:side * 1024 + layer * 512]
            g.remote_dma_fused([RemoteDMATransfer(dst_ids=ids, dma_engine_mask=m, remote_sem=T.sem["w%d%d" % (layer, side)],
                                                  srcs=[piece], dsts=[piece for d in dsts])], local_sem=T.sem.sent)
            sent[0] += _bits(m)

        need("g", t_sc)
        for s in range(1, NCH):
            i = (j + s) % NCH
            write(worker(i, s), T.land[:, BLK * (s - 1):BLK * s], T.send[:, lo[i]:lo[i] + BLK], T.sem["ar%d" % s])

    PH = [[T.ph00, T.ph01], [T.ph10, T.ph11]]
    PY = [T.py0, T.py1]
    hist = []
    order = [side, 1 - side]

    def ffn(n, x, x0, t_in, out):
        bb = n % 2
        old = hist[n - 2] if n >= 2 else None
        t1, tr, t2 = {}, {}, {}
        for e in order:
            need("p", t_in, wt[(1, e)])
            for f in range(FF):
                c0 = e * 1024 + f * 128
                t1[e] = done("p", P.matmul(PH[bb][e][:, CAP * f:CAP * f + CAP], T.w[:, c0:c0 + 128],
                                           x[:, x0 + CAP * e:x0 + CAP * e + CAP], True, True))
        for e in order:
            h = T.hs[:, (2 * bb + e) * 192:(2 * bb + e) * 192 + 192]
            q = "v" if e == order[0] else "s"
            need(q, t1[e], old[0][e] if old else None)
            if q == "v":
                tr[e] = ts(h, PH[bb][e][:, 0:192], 0.0, A.max)
            else:
                tr[e] = done("s", S.activation(out=h, in_=PH[bb][e][:, 0:192], func=F.Relu))
        for e in order:
            need("p", tr[e], wt[(2, e)], old[1] if old else None)
            for f in range(FF):
                c0 = e * 1024 + 512 + f * 128
                h0 = (2 * bb + e) * 192 + CAP * f
                t2[e] = done("p", P.matmul(PY[bb][:, CAP * e:CAP * e + CAP], T.w[:, c0:c0 + 128], T.hs[:, h0:h0 + CAP],
                                           f == 0, f == FF - 1))
        need("v", t2[order[1]])
        t_out = done("v", V.tensor_copy(out=out, in_=PY[bb][:, 0:BLK]))
        hist.append((t2, t_out))
        return t_out

    n = 0
    if is_rank:
        t_own = ffn(n, T.send, lo[j], t_sc, T.ret[:, lo[j]:lo[j] + BLK])
        n += 1
    for s in my_rounds:
        total["ar%d" % s] = n_off
        o0 = BLK * (s - 1)
        need("g", ffn(n, T.land, o0, ("ar%d" % s, n_off), T.outb[:, o0:o0 + BLK]))
        write(lane[((j - s) % NCH, die)], T.ret[:, lo[j]:lo[j] + BLK], T.outb[:, o0:o0 + BLK], T.sem.back)
        n += 1

    if is_rank:
        t_back = ("back", (NCH - 1) * n_off)
        total["back"] = t_back[1]
        half = TOK // 2
        need("v", t_back, t_own, t_gap)
        t_y0 = done("v", V.tensor_copy(out=T.ysb[:, 0:half], in_=T.ret[:, 0:WIN].indirect(T.off[:, 0:8])))
        need("s", t_back, t_own, t_gap)
        t_y1 = done("s", S.activation(out=T.ysb[:, half:TOK], in_=T.ret[:, 0:WIN].indirect(T.off[:, 8:16]), func=F.Copy))
        need("y", t_y0)
        g.sync.dma_start(T.y[:, 0:half], T.ysb[:, 0:half]).then_inc(T.sem.st, 16)
        need("s", t_y1)
        g.scalar.dma_start(T.y[:, half:TOK], T.ysb[:, half:TOK]).then_inc(T.sem.st, 16)
        total["st"] = 32

    total["sent"] = sent[0]
    for s in SEMAPHORES:
        if total.get(s, 0) > 0:
            need("g", (s, total[s]))
